import numpy as np
import ml_dtypes


def mxq(x, axis, fmt="e4m3"):
    dtype, down = {"e4m3": (ml_dtypes.float8_e4m3fn, 7), "e5m2": (ml_dtypes.float8_e5m2, 14)}[fmt]
    v = np.moveaxis(np.asarray(x, np.float32).astype(ml_dtypes.bfloat16).astype(np.float64), axis, -1)
    blocks = v.reshape(v.shape[:-1] + (-1, 32))
    amax = np.abs(blocks).max(-1, keepdims=True)
    byte = np.maximum(np.where(amax > 0, np.frexp(amax)[1] - 1 + 127, 0) - down, 1)
    scale = np.exp2(byte - 127.0)
    codes = (blocks / scale).astype(np.float32).astype(dtype).astype(np.float64)
    return np.moveaxis((codes * scale).reshape(v.shape), -1, axis)


WIDE = False


def mx_kscale(k):
    if not WIDE:
        return np.ones(k)
    levels = np.array([10, -10, 5, -5, 0])
    if k % 512:
        return np.exp2(np.random.permutation(np.resize(levels, k // 32))).repeat(32)
    a = np.empty((k // 512, 16))
    for p in range(k // 512):
        a[p, :8] = np.random.permutation(np.resize(levels, 8))
        for g in range(8):
            far = levels[np.abs(levels - a[p, g]) >= 10]
            a[p, g + 8] = far[np.random.randint(len(far))]
    return np.exp2(a.ravel()).repeat(32)


def f64(x):
    return np.asarray(x).astype(np.float64)


def striped(idx):
    return np.tile(idx.reshape(-1, 16).T, (8, 1)).astype(np.uint16)


def unstriped(offs):
    return offs[:16].T.reshape(-1).astype(np.int64)


E2M1 = np.array([0.0, 0.5, 1.0, 1.5, 2.0, 3.0, 4.0, 6.0, -0.0, -0.5, -1.0, -1.5, -2.0, -3.0, -4.0, -6.0])


def pack_weight(w, fmt):
    k, n = w.shape
    w = f64(np.asarray(w, np.float32).astype(ml_dtypes.bfloat16)).reshape(k // 32, 32, n)
    amax = np.abs(w).max(1)
    if fmt == "e4m3":
        byte = np.frexp(amax)[1] - 1 + 127 - 7
    else:
        mant, ex = np.frexp(amax / 6.0)
        byte = np.where(mant > 0.5, ex, ex - 1) + 127
    byte = np.clip(np.where(amax > 0, byte, 1), 1, 254)
    scaled = (w * np.exp2(127.0 - byte)[:, None, :]).reshape(k, n).astype(np.float32)
    by_word = np.ascontiguousarray(scaled.reshape(k // 512, 128, 4, n).transpose(0, 1, 3, 2))
    if fmt == "e4m3":
        words = by_word.astype(ml_dtypes.float8_e4m3fn).view(np.uint8)
    else:
        c = by_word.astype(ml_dtypes.float4_e2m1fn).view(np.uint8) & 0xF
        words = (c[..., 0::2] | (c[..., 1::2] << 4)).reshape(k // 512, 128, 2 * n)
    return np.ascontiguousarray(words), np.ascontiguousarray(byte.astype(np.uint8).reshape(k // 512, 16, n))


def unpack_weight(words, scales, fmt):
    g, _, n = scales.shape
    words = np.ascontiguousarray(words).reshape(g, 128, n, -1)
    if fmt == "e4m3":
        vals = words.view(ml_dtypes.float8_e4m3fn).astype(np.float64)
    else:
        nib = np.empty((g, 128, n, 4), np.uint8)
        nib[..., 0::2] = words & 0xF
        nib[..., 1::2] = words >> 4
        vals = E2M1[nib]
    vals = vals * np.repeat(np.exp2(scales.astype(np.float64) - 127.0), 8, axis=1)[..., None]
    return vals.transpose(0, 1, 3, 2).reshape(g * 512, n)


def relu2(v):
    return np.maximum(v, 0.0) ** 2


K, T, E, C, N = 1024, 640, 20, 128, 256
TOP = 4
M = 512


def by_expert(wq, xq):
    return np.concatenate([wq[e].T @ xq[:, e * C:(e + 1) * C] for e in range(E)], axis=1)


def setup_inputs():
    n = np.random.standard_normal
    s = mx_kscale(K)[:, None]
    deal = np.repeat(np.arange(E), C).reshape(TOP, T)[:, np.random.permutation(T)]
    deal = np.take_along_axis(deal, np.argsort(np.random.rand(TOP, T), axis=0), axis=0)
    for _ in range(8):
        s_, t_ = np.random.permutation(T).reshape(2, -1); r = np.random.randint(TOP, size=T // 2); x, y = deal[r, s_].copy(), deal[r, t_].copy()
        ok = ~((deal[:, s_] == y).any(0) | (deal[:, t_] == x).any(0)); deal[r[ok], s_[ok]] = y[ok]; deal[r[ok], t_[ok]] = x[ok]
    order = np.lexsort((np.random.rand(TOP * T), deal.reshape(-1)))
    slot_token = order % T; pos = np.empty(TOP * T, np.int64); pos[order] = np.arange(TOP * T); pos = pos.reshape(TOP, T)
    g = np.random.uniform(0.5, 1.5, (TOP, T)); g = g / g.sum(0)
    w = [pack_weight(m, "e2m1") for m in n((E, K, N)) / np.sqrt(K) / s[None]]
    r = mx_kscale(M)[:, None]
    return {
        "uT": (n((M, T)) * r).astype(np.float32),
        "wu": (n((M, K)) / np.sqrt(M) / r * s.T).astype(np.float32),
        "w_words": np.stack([m[0] for m in w]),
        "w_scales": np.stack([m[1] for m in w]),
        "b": (0.3 * n((N, E))).astype(np.float32),
        "gate": np.stack([np.tile(r, (N, 1)) for r in g]).astype(np.float32),
        "offs": striped(slot_token),
        "pos1": striped(pos[0]),
        "pos2": striped(pos[1]),
        "pos3": striped(pos[2]),
        "pos4": striped(pos[3]),
    }


def reference(uT, wu, w_words, w_scales, b, gate, offs, pos1, pos2, pos3, pos4):
    idx = unstriped(offs)
    w = np.stack([unpack_weight(w_words[e], w_scales[e], "e2m1") for e in range(E)])
    x = mxq(f64(wu), 0, "e4m3").T @ mxq(f64(uT), 0, "e4m3")
    xq = mxq(x[:, idx], 0, "e4m3")
    y = by_expert(w, xq)
    y = relu2(y + np.repeat(f64(b), C, axis=1))
    return sum(f64(gate[r]) * y[:, unstriped(p)] for r, p in enumerate((pos1, pos2, pos3, pos4)))

@@ -1,0 +1,236 @@
+from contextlib import ExitStack
+
+import concourse.mybir as mybir
+from concourse.masks import make_identity
+
+F32 = mybir.dt.float32
+BF16 = mybir.dt.bfloat16
+I32 = mybir.dt.int32
+U32 = mybir.dt.uint32
+U16 = mybir.dt.uint16
+U8 = mybir.dt.uint8
+FP8X4 = mybir.dt.float8_e4m3fn_x4
+FP4X4 = mybir.dt.float4_e2m1fn_x4
+ACT = mybir.ActivationFunctionType
+
+P = 128
+M, K, T, E, C, N, TOP = 512, 1024, 640, 20, 128, 256, 4
+SLOTS = E * C
+PASSES = K // 512
+BANK = 512
+WINDOW = 704
+TOKEN_CHUNKS = ((0, 256), (256, 256), (512, 128))
+SLOT_CHUNKS = (512, 512, 512, 512, 256, 256)
+EXPERTS_PER_LOAD = 5
+TOKEN_BLOCKS = T // P
+
+FLOPS = 2 * M * K * T + 2 * K * N * SLOTS
+
+
+def tile_moe_prv_lin_relu2_kernel(
+    tc, uT, wu, w_words, w_scales, b, gate, offs, pos1, pos2, pos3, pos4, out
+):
+    nc = tc.nc
+    with ExitStack() as ctx:
+        keep = ctx.enter_context(tc.tile_pool(name="keep", bufs=1))
+        ring = ctx.enter_context(tc.tile_pool(name="ring", bufs=3))
+        psum = ctx.enter_context(tc.psum_pool(name="psum", bufs=8))
+
+        def bank(name):
+            return psum.tile([P, BANK], F32, name=name, tag="bank")
+
+        planes = keep.tile([P, E * PASSES, N], U8, align_bytes=64)
+        nc.vector.memset(planes[:].bitcast(I32), 0)
+        gate_rows = keep.tile([P, T], F32)
+        nc.gpsimd.memset(gate_rows[:], 0.0)
+        ident = keep.tile([P, P], F32)
+        make_identity(nc, ident[:])
+        x_pairs = {}
+        for a in range(PASSES):
+            for h in range(2):
+                x_pairs[a, h] = keep.tile([P, WINDOW, 2], BF16, name=f"x_pairs{a}{h}")
+                nc.gpsimd.memset(x_pairs[a, h][:, T:, :], 0.0)
+
+        wu_rows = wu.rearrange("(p j) k -> p j k", j=4)
+        u_rows = uT.rearrange("(p j) t -> p j t", j=4)
+        wu_raw = [keep.tile([P, 4, 512], F32, name=f"wu_raw{a}") for a in range(PASSES)]
+        u_raw = [keep.tile([P, 4, n], F32, name=f"u_raw{i}") for i, (t0, n) in enumerate(TOKEN_CHUNKS)]
+        nc.sync.dma_start(out=wu_raw[0][:], in_=wu_rows[:, :, 0:512])
+        for i, (t0, n) in enumerate(TOKEN_CHUNKS):
+            nc.sync.dma_start(out=u_raw[i][:], in_=u_rows[:, :, t0:t0 + n])
+        offs_sb = keep.tile([P, SLOTS // 16], U16)
+        nc.sync.dma_start(offs_sb[:], offs)
+        nc.sync.dma_start(out=wu_raw[1][:], in_=wu_rows[:, :, 512:1024])
+        nc.sync.dma_start(out=gate_rows[0:TOP, :], in_=gate[:, 0, :])
+        bias = keep.tile([P, N // P, E], F32)
+        nc.sync.dma_start(out=bias[:], in_=b.rearrange("(nb p) e -> p nb e", p=P))
+
+        words = []
+
+        def load_words(g):
+            tile = keep.tile([P, EXPERTS_PER_LOAD * PASSES, 2 * N], U8, name=f"words{g}", align_bytes=64)
+            src = w_words[g * EXPERTS_PER_LOAD:(g + 1) * EXPERTS_PER_LOAD].rearrange("e a p c -> p (e a) c")
+            nc.sync.dma_start(out=tile[:].bitcast(I32), in_=src.bitcast(I32))
+            words.append(tile)
+
+        scale_rows = w_scales.rearrange("e a (q r) n -> r q (e a) n", r=4)
+        for r in range(4):
+            nc.sync.dma_start(out=planes[:].bitcast(I32)[r:P:32, :, :], in_=scale_rows[r].bitcast(I32))
+        for g in range(E // EXPERTS_PER_LOAD):
+            load_words(g)
+        pos_sb = []
+        for r, pos in enumerate((pos1, pos2, pos3, pos4)):
+            tile = keep.tile([P, T // 16], U16, name=f"pos_sb{r}")
+            nc.sync.dma_start(tile[:], pos)
+            pos_sb.append(tile)
+        gate_last = keep.tile([P, T], F32)
+        nc.sync.dma_start(out=gate_last[:], in_=gate[TOP - 1, N - P:N, :])
+
+        def quantise(grouped, n, name, pool, **kw):
+            codes = pool.tile([P, n], U32, name=name + "_codes", align_bytes=64, **kw)
+            scales = pool.tile([P, n], U8, name=name + "_scales", align_bytes=64, **kw)
+            nc.vector.quantize_mx(out=codes[:].bitcast(FP8X4), scales=scales[:], in_=grouped)
+            return codes, scales
+
+        def group_wu(a, copy, grouped):
+            copy(out=grouped.rearrange("p (d m j) -> p m j d", d=4, j=4), in_=wu_raw[a][:].rearrange("p j (m d) -> p m j d", d=4))
+            return grouped
+
+        def group_u(i, copy):
+            n = TOKEN_CHUNKS[i][1]
+            grouped = keep.tile([P, n, 4], BF16, name=f"u_grouped{i}", align_bytes=64)
+            copy(out=grouped[:].rearrange("p (c i) j -> p c j i", i=4), in_=u_raw[i][:].rearrange("p j (c i) -> p c j i", i=4))
+            return grouped[:].rearrange("p t j -> p (t j)")
+
+        def project(a, wq, i, h, copy):
+            t0, n = TOKEN_CHUNKS[i]
+            acc = bank("proj")
+            for e in range(2):
+                cols = slice((2 * h + e) * P, (2 * h + e + 1) * P)
+                nc.tensor.matmul_mx(
+                    out=acc[:, e * n:(e + 1) * n],
+                    lhsT=wq[0][:, cols].bitcast(FP8X4), lhsT_scale=wq[1][:, cols],
+                    rhs=uq[i][0][:].bitcast(FP8X4), rhs_scale=uq[i][1][:],
+                    start=True, stop=True)
+            copy(out=x_pairs[a, h][:, t0:t0 + n, :], in_=acc[:, 0:2 * n].rearrange("p (e t) -> p t e", e=2))
+
+        v_copy, s_copy = nc.vector.tensor_copy, nc.scalar.copy
+        wu0_grouped = keep.tile([P, 2048], BF16, align_bytes=64)
+        wq0 = quantise(group_wu(0, v_copy, wu0_grouped[:]), 512, "wu0", keep)
+        uq = []
+        for i, copy in enumerate((s_copy, v_copy, s_copy)):
+            uq.append(quantise(group_u(i, copy), TOKEN_CHUNKS[i][1], f"u{i}", keep))
+        for i in range(len(TOKEN_CHUNKS)):
+            project(0, wq0, i, 0, v_copy)
+            project(0, wq0, i, 1, s_copy)
+
+        gate_cols = keep.tile([P, TOKEN_BLOCKS, TOP], F32)
+        for first, count in ((0, 4), (4, 1)):
+            turned = bank("gate_turned")
+            for tb in range(count):
+                nc.tensor.transpose(turned[:, tb * P:(tb + 1) * P], gate_rows[:, (first + tb) * P:(first + tb + 1) * P], ident[:])
+            nc.scalar.activation(gate_cols[:, first:first + count, :],
+                                 turned[:, 0:count * P].rearrange("p (b n) -> p b n", n=P)[:, :, 0:TOP], ACT.Copy)
+
+        y = [keep.tile([P, SLOTS], F32, name=f"y{nb}") for nb in range(N // P)]
+        starts = [sum(SLOT_CHUNKS[:c]) for c in range(len(SLOT_CHUNKS))]
+
+        last = len(SLOT_CHUNKS) - 1
+        units = [(0, 0), (1, 0), (0, 1), (1, 1)]
+        for c in range(2, last + 1):
+            units.extend([(c, 0), (c, 1)])
+        between = {3: [(0, 0)], 4: [(1, 0)], 5: [(0, 1)], 6: [(2, 0)], 7: [(1, 1)], 8: [(3, 0)], 10: [(4, 0)],
+                   11: [(5, 0), (2, 1), (3, 1), (4, 1), (5, 1)]}
+        stage = [keep.tile([P, 2 * BANK], U32, name=f"stage{i}", align_bytes=64) for i in range(3)]
+        picked = [keep.tile([P, 2 * BANK], U32, name=f"picked{i}", align_bytes=64) for i in range(2)]
+        xq = {}
+
+        def gather(u):
+            c, a = units[u]
+            s0, n = starts[c], SLOT_CHUNKS[c]
+            for h in range(2):
+                window = x_pairs[a, h][:].rearrange("p t e -> p (t e)").bitcast(U32)
+                nc.vector.tensor_copy(picked[u % 2][:, h * n:(h + 1) * n], window.indirect(offs_sb[:, s0 // 16:(s0 + n) // 16]))
+
+        def weave(u):
+            n = SLOT_CHUNKS[units[u][0]]
+            nc.scalar.copy(out=stage[u % 3][:, 0:2 * n].rearrange("p (s h) -> p s h", h=2),
+                           in_=picked[u % 2][:, 0:2 * n].rearrange("p (h s) -> p s h", h=2))
+
+        def quantise_unit(u):
+            c, a = units[u]
+            n = SLOT_CHUNKS[c]
+            xq[c, a] = quantise(stage[u % 3][:, 0:2 * n].bitcast(BF16), n, f"slot{c}{a}", keep)
+
+        def experts(c, nb, relu):
+            s0, n = starts[c], SLOT_CHUNKS[c]
+            acc = bank("expert")
+            for i in range(n // C):
+                e = s0 // C + i
+                g, le = divmod(e, EXPERTS_PER_LOAD)
+                for a in range(PASSES):
+                    nc.tensor.matmul_mx(
+                        out=acc[:, i * C:(i + 1) * C],
+                        lhsT=words[g][:, le * PASSES + a, nb * 2 * P:(nb + 1) * 2 * P].bitcast(FP4X4),
+                        lhsT_scale=planes[:, e * PASSES + a, nb * P:(nb + 1) * P],
+                        rhs=xq[c, a][0][:, i * C:(i + 1) * C].bitcast(FP8X4),
+                        rhs_scale=xq[c, a][1][:, i * C:(i + 1) * C],
+                        start=(a == 0), stop=(a == PASSES - 1))
+            for i in range(n // C):
+                e = s0 // C + i
+                nc.scalar.activation(relu[:, i * C:(i + 1) * C], acc[:, i * C:(i + 1) * C], ACT.Relu,
+                                     bias=bias[:, nb, e:e + 1])
+            nc.scalar.activation(y[nb][:, s0:s0 + n], relu[:, 0:n], ACT.Square)
+
+        wq1_in = group_wu(1, s_copy, picked[1][:].bitcast(BF16))
+        for u in range(len(units) + 1):
+            if u < len(units):
+                if u == 1:
+                    wq1 = quantise(wq1_in, 512, "wu1", keep)
+                    for h in range(2):
+                        for i in range(len(TOKEN_CHUNKS)):
+                            project(1, wq1, i, h, s_copy)
+                gather(u)
+                weave(u)
+            if u > 0:
+                quantise_unit(u - 1)
+            if u == len(units):
+                for c, nb in between[u - 1]:
+                    relu = ring.tile([P, BANK], F32, name="relu")
+                    experts(c, nb, relu[:])
+            elif u < len(units) - 1:
+                for c, nb in between.get(u, []):
+                    experts(c, nb, stage[(u + 1) % 3][:].bitcast(F32))
+
+        groups = ((0, 4), (4, 1))
+        for nb in range(N // P):
+            final = nb == N // P - 1
+            turned_choices = TOP - 1 if final else TOP
+            total = [bank(f"total{i}") for i in range(len(groups))]
+            for r in range(turned_choices):
+                fetched = ring.tile([P, T], F32, name="fetched")
+                nc.vector.tensor_copy(fetched[:], y[nb][:].indirect(pos_sb[r][:]))
+                for gi, (first, count) in enumerate(groups):
+                    turned = bank("turned")
+                    for tb in range(count):
+                        nc.tensor.transpose(turned[:, tb * P:(tb + 1) * P],
+                                            fetched[:, (first + tb) * P:(first + tb + 1) * P], ident[:])
+                    weighted = ring.tile([P, BANK], F32, name="weighted")
+                    for tb in range(count):
+                        nc.scalar.activation(weighted[:, tb * P:(tb + 1) * P], turned[:, tb * P:(tb + 1) * P], ACT.Copy,
+                                             scale=gate_cols[:, first + tb, r:r + 1])
+                    for tb in range(count):
+                        nc.tensor.matmul(total[gi][:, tb * P:(tb + 1) * P], weighted[:, tb * P:(tb + 1) * P], ident[:],
+                                         start=(r == 0 and tb == 0), stop=(r == turned_choices - 1 and tb == count - 1),
+                                         is_transpose=True)
+            for gi, (first, count) in enumerate(groups):
+                t0, n = first * P, count * P
+                result = ring.tile([P, BANK], F32, name="result")
+                if final:
+                    product = ring.tile([P, BANK], F32, name="product")
+                    nc.vector.tensor_tensor(product[:, 0:n], y[nb][:].indirect(pos_sb[TOP - 1][:, t0 // 16:(t0 + n) // 16]),
+                                            gate_last[:, t0:t0 + n], mybir.AluOpType.mult)
+                    nc.vector.tensor_tensor(result[:, 0:n], total[gi][:, 0:n], product[:, 0:n], mybir.AluOpType.add)
+                else:
+                    nc.scalar.copy(out=result[:, 0:n], in_=total[gi][:, 0:n])
+                nc.sync.dma_start(out=out[nb * P:(nb + 1) * P, t0:t0 + n], in_=result[:, 0:n])

@@ -53,14 +53,15 @@ def tile_moe_prv_lin_relu2_kernel(
 
         wu_rows = wu.rearrange("(p j) k -> p j k", j=4)
         u_rows = uT.rearrange("(p j) t -> p j t", j=4)
-        wu_raw = [keep.tile([P, 4, 512], F32, name=f"wu_raw{a}") for a in range(PASSES)]
+        wu_raw = [keep.tile([P, 4, 256], F32, name=f"wu_raw{i}") for i in range(2)] + [keep.tile([P, 4, 512], F32, name="wu_raw2")]
         u_raw = [keep.tile([P, 4, n], F32, name=f"u_raw{i}") for i, (t0, n) in enumerate(TOKEN_CHUNKS)]
-        nc.sync.dma_start(out=wu_raw[0][:], in_=wu_rows[:, :, 0:512])
+        for i in range(2):
+            nc.sync.dma_start(out=wu_raw[i][:], in_=wu_rows[:, :, 256 * i:256 * (i + 1)])
         for i, (t0, n) in enumerate(TOKEN_CHUNKS):
             nc.sync.dma_start(out=u_raw[i][:], in_=u_rows[:, :, t0:t0 + n])
         offs_sb = keep.tile([P, SLOTS // 16], U16)
         nc.sync.dma_start(offs_sb[:], offs)
-        nc.sync.dma_start(out=wu_raw[1][:], in_=wu_rows[:, :, 512:1024])
+        nc.sync.dma_start(out=wu_raw[2][:], in_=wu_rows[:, :, 512:1024])
         nc.sync.dma_start(out=gate_rows[0:TOP, :], in_=gate[:, 0, :])
         bias = keep.tile([P, N // P, E], F32)
         nc.sync.dma_start(out=bias[:], in_=b.rearrange("(nb p) e -> p nb e", p=P))
@@ -92,9 +93,10 @@ def tile_moe_prv_lin_relu2_kernel(
             nc.vector.quantize_mx(out=codes[:].bitcast(FP8X4), scales=scales[:], in_=grouped)
             return codes, scales
 
-        def group_wu(a, copy, grouped):
-            copy(out=grouped.rearrange("p (d m j) -> p m j d", d=4, j=4), in_=wu_raw[a][:].rearrange("p j (m d) -> p m j d", d=4))
-            return grouped
+        def group_wu(raw, m0, copy, grouped):
+            count = raw.shape[2] // 4
+            copy(out=grouped.rearrange("p (d m j) -> p m j d", d=4, j=4)[:, m0:m0 + count, :, :],
+                 in_=raw[:].rearrange("p j (m d) -> p m j d", d=4))
 
         def group_u(i, copy):
             n = TOKEN_CHUNKS[i][1]
@@ -116,12 +118,15 @@ def tile_moe_prv_lin_relu2_kernel(
 
         v_copy, s_copy = nc.vector.tensor_copy, nc.scalar.copy
         wu0_grouped = keep.tile([P, 2048], BF16, align_bytes=64)
-        wq0 = quantise(group_wu(0, v_copy, wu0_grouped[:]), 512, "wu0", keep)
+        for i in range(2):
+            group_wu(wu_raw[i], 64 * i, v_copy, wu0_grouped[:])
+        wq0 = quantise(wu0_grouped[:], 512, "wu0", keep)
         uq = []
         for i, copy in enumerate((s_copy, v_copy, s_copy)):
             uq.append(quantise(group_u(i, copy), TOKEN_CHUNKS[i][1], f"u{i}", keep))
+        for i, copy in enumerate((s_copy, v_copy, s_copy)):
+            project(0, wq0, i, 0, copy)
         for i in range(len(TOKEN_CHUNKS)):
-            project(0, wq0, i, 0, v_copy)
             project(0, wq0, i, 1, s_copy)
 
         gate_cols = keep.tile([P, TOKEN_BLOCKS, TOP], F32)
@@ -139,10 +144,15 @@ def tile_moe_prv_lin_relu2_kernel(
         units = [(0, 0), (1, 0), (0, 1), (1, 1)]
         for c in range(2, last + 1):
             units.extend([(c, 0), (c, 1)])
-        between = {3: [(0, 0)], 4: [(1, 0)], 5: [(0, 1)], 6: [(2, 0)], 7: [(1, 1)], 8: [(3, 0)], 10: [(4, 0)],
-                   11: [(5, 0), (2, 1), (3, 1), (4, 1), (5, 1)]}
-        stage = [keep.tile([P, 2 * BANK], U32, name=f"stage{i}", align_bytes=64) for i in range(3)]
-        picked = [keep.tile([P, 2 * BANK], U32, name=f"picked{i}", align_bytes=64) for i in range(2)]
+        between = {3: [(0, 0)], 4: [(1, 0)], 5: [(0, 1)], 6: [(2, 0)], 7: [(1, 1)], 8: [(2, 1)], 9: [(3, 0)]}
+        stage = [keep.tile([P, 2 * BANK], U32, name=f"stage{i}", align_bytes=64) for i in range(2)]
+        picked = [keep.tile([P, 3 * BANK], U32, name=f"picked{i}", align_bytes=64) for i in range(2)]
+        end = len(units) - 1
+
+        def woven(u):
+            n = SLOT_CHUNKS[units[u][0]]
+            tile = picked[(end - 1) % 2] if u == end else stage[0] if u == 1 else stage[(u + 1) % 2] if u > 1 else stage[0]
+            return tile[:, 0:2 * n]
         xq = {}
 
         def gather(u):
@@ -154,15 +164,19 @@ def tile_moe_prv_lin_relu2_kernel(
 
         def weave(u):
             n = SLOT_CHUNKS[units[u][0]]
-            nc.scalar.copy(out=stage[u % 3][:, 0:2 * n].rearrange("p (s h) -> p s h", h=2),
+            nc.scalar.copy(out=woven(u).rearrange("p (s h) -> p s h", h=2),
                            in_=picked[u % 2][:, 0:2 * n].rearrange("p (h s) -> p s h", h=2))
 
         def quantise_unit(u):
             c, a = units[u]
             n = SLOT_CHUNKS[c]
-            xq[c, a] = quantise(stage[u % 3][:, 0:2 * n].bitcast(BF16), n, f"slot{c}{a}", keep)
+            xq[c, a] = quantise(woven(u).bitcast(BF16), n, f"slot{c}{a}", keep)
 
-        def experts(c, nb, relu):
+        def relu_tile():
+            tile = ring.tile([P, 2 * C], F32, name="relu")
+            return tile[:]
+
+        def experts(c, nb, first, second=None, on_vector=False):
             s0, n = starts[c], SLOT_CHUNKS[c]
             acc = bank("expert")
             for i in range(n // C):
@@ -176,42 +190,61 @@ def tile_moe_prv_lin_relu2_kernel(
                         rhs=xq[c, a][0][:, i * C:(i + 1) * C].bitcast(FP8X4),
                         rhs_scale=xq[c, a][1][:, i * C:(i + 1) * C],
                         start=(a == 0), stop=(a == PASSES - 1))
+            halves = [first, relu_tile() if second is None else second] if n > 2 * C else [first]
             for i in range(n // C):
                 e = s0 // C + i
-                nc.scalar.activation(relu[:, i * C:(i + 1) * C], acc[:, i * C:(i + 1) * C], ACT.Relu,
-                                     bias=bias[:, nb, e:e + 1])
-            nc.scalar.activation(y[nb][:, s0:s0 + n], relu[:, 0:n], ACT.Square)
+                relu = halves[i // 2][:, (i % 2) * C:(i % 2 + 1) * C]
+                if on_vector:
+                    nc.vector.tensor_scalar(relu, acc[:, i * C:(i + 1) * C], bias[:, nb, e:e + 1], 0.0,
+                                            mybir.AluOpType.add, mybir.AluOpType.max)
+                else:
+                    nc.scalar.activation(relu, acc[:, i * C:(i + 1) * C], ACT.Relu, bias=bias[:, nb, e:e + 1])
+            width = max(n // 2, C)
+            for i in range(n // width):
+                src = halves[i][:, 0:width] if n > 2 * C else first[:, i * width:(i + 1) * width]
+                dst = y[nb][:, s0 + i * width:s0 + (i + 1) * width]
+                if on_vector:
+                    nc.vector.tensor_tensor(dst, src, src, mybir.AluOpType.mult)
+                else:
+                    nc.scalar.activation(dst, src, ACT.Square)
 
-        wq1_in = group_wu(1, s_copy, picked[1][:].bitcast(BF16))
-        for u in range(len(units) + 1):
-            if u < len(units):
-                if u == 1:
-                    wq1 = quantise(wq1_in, 512, "wu1", keep)
-                    for h in range(2):
-                        for i in range(len(TOKEN_CHUNKS)):
-                            project(1, wq1, i, h, s_copy)
-                gather(u)
-                weave(u)
-            if u > 0:
+        wq1_in = picked[1][:, BANK:3 * BANK].bitcast(BF16)
+        group_wu(wu_raw[2], 0, s_copy, wq1_in)
+        for u in range(len(units)):
+            if u == 1:
+                wq1 = quantise(wq1_in, 512, "wu1", keep)
+                for h in range(2):
+                    for i in range(len(TOKEN_CHUNKS)):
+                        project(1, wq1, i, h, v_copy if (h, i) == (0, 9) else s_copy)
+            gather(u)
+            if u == 1:
+                quantise_unit(0)
+            weave(u)
+            if u > 1:
                 quantise_unit(u - 1)
-            if u == len(units):
-                for c, nb in between[u - 1]:
-                    relu = ring.tile([P, BANK], F32, name="relu")
-                    experts(c, nb, relu[:])
-            elif u < len(units) - 1:
-                for c, nb in between.get(u, []):
-                    experts(c, nb, stage[(u + 1) % 3][:].bitcast(F32))
+            for c, nb in between.get(u, []):
+                experts(c, nb, woven(u + 1).bitcast(F32))
+        spare = picked[end % 2][:].bitcast(F32)
+        experts(last - 1, 0, spare[:, 0:256])
+        quantise_unit(end)
+        experts(last, 0, spare[:, 256:512])
+        after = woven(end).bitcast(F32)
+        experts(last - 2, 1, after[:, 0:256], after[:, 256:512], on_vector=True)
+        for c in (last - 1, last):
+            experts(c, 1, spare[:, 256:512])
 
         groups = ((0, 4), (4, 1))
+        turn_banks = [[bank("turned0"), bank("turned1")], [bank("turned2"), bank("turned3")]]
+        fetch_ring = [keep.tile([P, T], F32, name=f"fetched{i}") for i in range(3)]
         for nb in range(N // P):
             final = nb == N // P - 1
             turned_choices = TOP - 1 if final else TOP
             total = [bank(f"total{i}") for i in range(len(groups))]
             for r in range(turned_choices):
-                fetched = ring.tile([P, T], F32, name="fetched")
+                fetched = fetch_ring[(nb * TOP + r) % 3]
                 nc.vector.tensor_copy(fetched[:], y[nb][:].indirect(pos_sb[r][:]))
                 for gi, (first, count) in enumerate(groups):
-                    turned = bank("turned")
+                    turned = turn_banks[gi][(nb * TOP + r) % len(turn_banks[gi])]
                     for tb in range(count):
                         nc.tensor.transpose(turned[:, tb * P:(tb + 1) * P],
                                             fetched[:, (first + tb) * P:(first + tb + 1) * P], ident[:])
@@ -227,10 +260,10 @@ def tile_moe_prv_lin_relu2_kernel(
                 t0, n = first * P, count * P
                 result = ring.tile([P, BANK], F32, name="result")
                 if final:
-                    product = ring.tile([P, BANK], F32, name="product")
-                    nc.vector.tensor_tensor(product[:, 0:n], y[nb][:].indirect(pos_sb[TOP - 1][:, t0 // 16:(t0 + n) // 16]),
+                    product = fetch_ring[(nb * TOP + TOP - 1) % 3][:, t0:t0 + n]
+                    nc.vector.tensor_tensor(product, y[nb][:].indirect(pos_sb[TOP - 1][:, t0 // 16:(t0 + n) // 16]),
                                             gate_last[:, t0:t0 + n], mybir.AluOpType.mult)
-                    nc.vector.tensor_tensor(result[:, 0:n], total[gi][:, 0:n], product[:, 0:n], mybir.AluOpType.add)
+                    nc.vector.tensor_tensor(result[:, 0:n], total[gi][:, 0:n], product, mybir.AluOpType.add)
                 else:
                     nc.scalar.copy(out=result[:, 0:n], in_=total[gi][:, 0:n])
                 nc.sync.dma_start(out=out[nb * P:(nb + 1) * P, t0:t0 + n], in_=result[:, 0:n])

@@ -43,6 +43,7 @@ def tile_moe_prv_lin_relu2_kernel(
         nc.vector.memset(planes[:].bitcast(I32), 0)
         gate_rows = keep.tile([P, T], F32)
         nc.gpsimd.memset(gate_rows[:], 0.0)
+        nc.scalar.dma_start(out=gate_rows[0:TOP, :], in_=gate[:, 0, :])
         ident = keep.tile([P, P], F32)
         make_identity(nc, ident[:])
         x_pairs = {}
@@ -62,7 +63,6 @@ def tile_moe_prv_lin_relu2_kernel(
         offs_sb = keep.tile([P, SLOTS // 16], U16)
         nc.sync.dma_start(offs_sb[:], offs)
         nc.sync.dma_start(out=wu_raw[2][:], in_=wu_rows[:, :, 512:1024])
-        nc.sync.dma_start(out=gate_rows[0:TOP, :], in_=gate[:, 0, :])
         bias = keep.tile([P, N // P, E], F32)
         nc.sync.dma_start(out=bias[:], in_=b.rearrange("(nb p) e -> p nb e", p=P))
 
@@ -86,6 +86,14 @@ def tile_moe_prv_lin_relu2_kernel(
             pos_sb.append(tile)
         gate_last = keep.tile([P, T], F32)
         nc.sync.dma_start(out=gate_last[:], in_=gate[TOP - 1, N - P:N, :])
+
+        gate_cols = keep.tile([P, TOKEN_BLOCKS, TOP], F32)
+        for first, count in ((0, 4), (4, 1)):
+            turned = bank("gate_turned")
+            for tb in range(count):
+                nc.tensor.transpose(turned[:, tb * P:(tb + 1) * P], gate_rows[:, (first + tb) * P:(first + tb + 1) * P], ident[:])
+            nc.scalar.activation(gate_cols[:, first:first + count, :],
+                                 turned[:, 0:count * P].rearrange("p (b n) -> p b n", n=P)[:, :, 0:TOP], ACT.Copy)
 
         def quantise(grouped, n, name, pool, **kw):
             codes = pool.tile([P, n], U32, name=name + "_codes", align_bytes=64, **kw)
@@ -129,29 +137,21 @@ def tile_moe_prv_lin_relu2_kernel(
         for i in range(len(TOKEN_CHUNKS)):
             project(0, wq0, i, 1, s_copy)
 
-        gate_cols = keep.tile([P, TOKEN_BLOCKS, TOP], F32)
-        for first, count in ((0, 4), (4, 1)):
-            turned = bank("gate_turned")
-            for tb in range(count):
-                nc.tensor.transpose(turned[:, tb * P:(tb + 1) * P], gate_rows[:, (first + tb) * P:(first + tb + 1) * P], ident[:])
-            nc.scalar.activation(gate_cols[:, first:first + count, :],
-                                 turned[:, 0:count * P].rearrange("p (b n) -> p b n", n=P)[:, :, 0:TOP], ACT.Copy)
-
         y = [keep.tile([P, SLOTS], F32, name=f"y{nb}") for nb in range(N // P)]
         starts = [sum(SLOT_CHUNKS[:c]) for c in range(len(SLOT_CHUNKS))]
 
         last = len(SLOT_CHUNKS) - 1
-        units = [(0, 0), (1, 0), (0, 1), (1, 1)]
-        for c in range(2, last + 1):
+        units = [(0, 0), (1, 0), (2, 0), (0, 1), (1, 1), (2, 1)]
+        for c in range(3, last + 1):
             units.extend([(c, 0), (c, 1)])
-        between = {3: [(0, 0)], 4: [(1, 0)], 5: [(0, 1)], 6: [(2, 0)], 7: [(1, 1)], 8: [(2, 1)], 9: [(3, 0)]}
+        between = {4: [(0, 0)], 5: [(1, 0)], 6: [(2, 0)], 7: [(0, 1)], 9: [(3, 0)]}
         stage = [keep.tile([P, 2 * BANK], U32, name=f"stage{i}", align_bytes=64) for i in range(2)]
         picked = [keep.tile([P, 3 * BANK], U32, name=f"picked{i}", align_bytes=64) for i in range(2)]
         end = len(units) - 1
 
         def woven(u):
             n = SLOT_CHUNKS[units[u][0]]
-            tile = picked[(end - 1) % 2] if u == end else stage[0] if u == 1 else stage[(u + 1) % 2] if u > 1 else stage[0]
+            tile = picked[(end - 1) % 2] if u == end else stage[u % 2]
             return tile[:, 0:2 * n]
         xq = {}
 
@@ -217,10 +217,8 @@ def tile_moe_prv_lin_relu2_kernel(
                     for i in range(len(TOKEN_CHUNKS)):
                         project(1, wq1, i, h, v_copy if (h, i) == (0, 9) else s_copy)
             gather(u)
-            if u == 1:
-                quantise_unit(0)
             weave(u)
-            if u > 1:
+            if u > 0:
                 quantise_unit(u - 1)
             for c, nb in between.get(u, []):
                 experts(c, nb, woven(u + 1).bitcast(F32))
@@ -229,22 +227,23 @@ def tile_moe_prv_lin_relu2_kernel(
         quantise_unit(end)
         experts(last, 0, spare[:, 256:512])
         after = woven(end).bitcast(F32)
-        experts(last - 2, 1, after[:, 0:256], after[:, 256:512], on_vector=True)
-        for c in (last - 1, last):
-            experts(c, 1, spare[:, 256:512])
+        experts(3, 1, after[:, 0:256], after[:, 256:512], on_vector=True)
+        for c in (1, 2, 4, 5):
+            experts(c, 1, spare[:, 256:512], spare[:, 512:768])
 
         groups = ((0, 4), (4, 1))
         turn_banks = [[bank("turned0"), bank("turned1")], [bank("turned2"), bank("turned3")]]
+        products = keep.tile([P, T], F32)
         fetch_ring = [keep.tile([P, T], F32, name=f"fetched{i}") for i in range(3)]
         for nb in range(N // P):
-            final = nb == N // P - 1
-            turned_choices = TOP - 1 if final else TOP
+            final = True
+            turned_choices = TOP - 1
             total = [bank(f"total{i}") for i in range(len(groups))]
             for r in range(turned_choices):
-                fetched = fetch_ring[(nb * TOP + r) % 3]
+                fetched = fetch_ring[r]
                 nc.vector.tensor_copy(fetched[:], y[nb][:].indirect(pos_sb[r][:]))
                 for gi, (first, count) in enumerate(groups):
-                    turned = turn_banks[gi][(nb * TOP + r) % len(turn_banks[gi])]
+                    turned = turn_banks[gi][(nb * (TOP - 1) + r) % 2]
                     for tb in range(count):
                         nc.tensor.transpose(turned[:, tb * P:(tb + 1) * P],
                                             fetched[:, (first + tb) * P:(first + tb + 1) * P], ident[:])
@@ -260,7 +259,7 @@ def tile_moe_prv_lin_relu2_kernel(
                 t0, n = first * P, count * P
                 result = ring.tile([P, BANK], F32, name="result")
                 if final:
-                    product = fetch_ring[(nb * TOP + TOP - 1) % 3][:, t0:t0 + n]
+                    product = products[:, t0:t0 + n]
                     nc.vector.tensor_tensor(product, y[nb][:].indirect(pos_sb[TOP - 1][:, t0 // 16:(t0 + n) // 16]),
                                             gate_last[:, t0:t0 + n], mybir.AluOpType.mult)
                     nc.vector.tensor_tensor(result[:, 0:n], total[gi][:, 0:n], product, mybir.AluOpType.add)

@@ -12,17 +12,26 @@ U8 = mybir.dt.uint8
 FP8X4 = mybir.dt.float8_e4m3fn_x4
 FP4X4 = mybir.dt.float4_e2m1fn_x4
 ACT = mybir.ActivationFunctionType
+ALU = mybir.AluOpType
 
 P = 128
+PACK = 4
+PASS = P * PACK
+LIST_ROWS = 16
+BANK = 512
 M, K, T, E, C, N, TOP = 512, 1024, 640, 20, 128, 256, 4
 SLOTS = E * C
-PASSES = K // 512
-BANK = 512
-WINDOW = 704
+PASSES = K // PASS
+ROW_BLOCKS = N // P
+TOKEN_BLOCKS = T // P
+
 TOKEN_CHUNKS = ((0, 256), (256, 256), (512, 128))
 SLOT_CHUNKS = (512, 512, 512, 512, 256, 256)
+LEAD = 3
+WINDOW = 704
 EXPERTS_PER_LOAD = 5
-TOKEN_BLOCKS = T // P
+GATE_STEP = 36
+TOKEN_GROUPS = ((0, 4), (4, 1))
 
 FLOPS = 2 * M * K * T + 2 * K * N * SLOTS
 
@@ -35,15 +44,16 @@ def tile_moe_prv_lin_relu2_kernel(
         keep = ctx.enter_context(tc.tile_pool(name="keep", bufs=1))
         ring = ctx.enter_context(tc.tile_pool(name="ring", bufs=3))
         psum = ctx.enter_context(tc.psum_pool(name="psum", bufs=8))
+        v_copy, s_copy = nc.vector.tensor_copy, nc.scalar.copy
 
         def bank(name):
             return psum.tile([P, BANK], F32, name=name, tag="bank")
 
-        planes = keep.tile([P, E * PASSES, N], U8, align_bytes=64)
-        nc.vector.memset(planes[:].bitcast(I32), 0)
-        gate_rows = keep.tile([P, T], F32)
-        nc.gpsimd.memset(gate_rows[:], 0.0)
-        nc.scalar.dma_start(out=gate_rows[0:TOP, :], in_=gate[:, 0, :])
+        w_scale_sb = keep.tile([P, E * PASSES, N], U8, align_bytes=64)
+        nc.vector.memset(w_scale_sb[:].bitcast(I32), 0)
+        gate_rows = keep.tile([P, P], F32)
+        gate_pieces = gate.rearrange("r n (b t) -> (r n b) t", t=P)
+        nc.sync.dma_start(out=gate_rows[:], in_=gate_pieces[0:GATE_STEP * P:GATE_STEP, :])
         ident = keep.tile([P, P], F32)
         make_identity(nc, ident[:])
         x_pairs = {}
@@ -52,217 +62,219 @@ def tile_moe_prv_lin_relu2_kernel(
                 x_pairs[a, h] = keep.tile([P, WINDOW, 2], BF16, name=f"x_pairs{a}{h}")
                 nc.gpsimd.memset(x_pairs[a, h][:, T:, :], 0.0)
 
-        wu_rows = wu.rearrange("(p j) k -> p j k", j=4)
-        u_rows = uT.rearrange("(p j) t -> p j t", j=4)
-        wu_raw = [keep.tile([P, 4, 256], F32, name=f"wu_raw{i}") for i in range(2)] + [keep.tile([P, 4, 512], F32, name="wu_raw2")]
-        u_raw = [keep.tile([P, 4, n], F32, name=f"u_raw{i}") for i, (t0, n) in enumerate(TOKEN_CHUNKS)]
+        wu_rows = wu.rearrange("(p j) k -> p j k", j=PACK)
+        u_rows = uT.rearrange("(p j) t -> p j t", j=PACK)
+        half = PASS // 2
+        wu0_raw = [keep.tile([P, PACK, half], F32, name=f"wu0_raw{i}") for i in range(2)]
+        wu1_raw = keep.tile([P, PACK, PASS], F32)
+        u_raw = [keep.tile([P, PACK, n], F32, name=f"u_raw{i}") for i, (t0, n) in enumerate(TOKEN_CHUNKS)]
         for i in range(2):
-            nc.sync.dma_start(out=wu_raw[i][:], in_=wu_rows[:, :, 256 * i:256 * (i + 1)])
+            nc.sync.dma_start(out=wu0_raw[i][:], in_=wu_rows[:, :, half * i:half * (i + 1)])
         for i, (t0, n) in enumerate(TOKEN_CHUNKS):
             nc.sync.dma_start(out=u_raw[i][:], in_=u_rows[:, :, t0:t0 + n])
-        offs_sb = keep.tile([P, SLOTS // 16], U16)
+        offs_sb = keep.tile([P, SLOTS // LIST_ROWS], U16)
         nc.sync.dma_start(offs_sb[:], offs)
-        nc.sync.dma_start(out=wu_raw[2][:], in_=wu_rows[:, :, 512:1024])
-        bias = keep.tile([P, N // P, E], F32)
+        nc.sync.dma_start(out=wu1_raw[:], in_=wu_rows[:, :, PASS:2 * PASS])
+        bias = keep.tile([P, ROW_BLOCKS, E], F32)
         nc.sync.dma_start(out=bias[:], in_=b.rearrange("(nb p) e -> p nb e", p=P))
-
-        words = []
-
-        def load_words(g):
-            tile = keep.tile([P, EXPERTS_PER_LOAD * PASSES, 2 * N], U8, name=f"words{g}", align_bytes=64)
-            src = w_words[g * EXPERTS_PER_LOAD:(g + 1) * EXPERTS_PER_LOAD].rearrange("e a p c -> p (e a) c")
-            nc.sync.dma_start(out=tile[:].bitcast(I32), in_=src.bitcast(I32))
-            words.append(tile)
 
         scale_rows = w_scales.rearrange("e a (q r) n -> r q (e a) n", r=4)
         for r in range(4):
-            nc.sync.dma_start(out=planes[:].bitcast(I32)[r:P:32, :, :], in_=scale_rows[r].bitcast(I32))
+            nc.sync.dma_start(out=w_scale_sb[:].bitcast(I32)[r:P:32, :, :], in_=scale_rows[r].bitcast(I32))
+        w_word_sb = []
         for g in range(E // EXPERTS_PER_LOAD):
-            load_words(g)
+            words = keep.tile([P, EXPERTS_PER_LOAD * PASSES, 2 * N], U8, name=f"words{g}", align_bytes=64)
+            src = w_words[g * EXPERTS_PER_LOAD:(g + 1) * EXPERTS_PER_LOAD].rearrange("e a p c -> p (e a) c")
+            nc.sync.dma_start(out=words[:].bitcast(I32), in_=src.bitcast(I32))
+            w_word_sb.append(words)
         pos_sb = []
         for r, pos in enumerate((pos1, pos2, pos3, pos4)):
-            tile = keep.tile([P, T // 16], U16, name=f"pos_sb{r}")
-            nc.sync.dma_start(tile[:], pos)
-            pos_sb.append(tile)
+            pos_tile = keep.tile([P, T // LIST_ROWS], U16, name=f"pos_sb{r}")
+            nc.sync.dma_start(pos_tile[:], pos)
+            pos_sb.append(pos_tile)
         gate_last = keep.tile([P, T], F32)
         nc.sync.dma_start(out=gate_last[:], in_=gate[TOP - 1, N - P:N, :])
 
-        gate_cols = keep.tile([P, TOKEN_BLOCKS, TOP], F32)
-        for first, count in ((0, 4), (4, 1)):
-            turned = bank("gate_turned")
-            for tb in range(count):
-                nc.tensor.transpose(turned[:, tb * P:(tb + 1) * P], gate_rows[:, (first + tb) * P:(first + tb + 1) * P], ident[:])
-            nc.scalar.activation(gate_cols[:, first:first + count, :],
-                                 turned[:, 0:count * P].rearrange("p (b n) -> p b n", n=P)[:, :, 0:TOP], ACT.Copy)
+        gate_cols = keep.tile([P, P], F32)
+        gate_turned = bank("gate_turned")
+        nc.tensor.transpose(gate_turned[:, 0:P], gate_rows[:], ident[:])
+        nc.scalar.activation(gate_cols[:], gate_turned[:, 0:P], ACT.Copy)
 
-        def quantise(grouped, n, name, pool, **kw):
-            codes = pool.tile([P, n], U32, name=name + "_codes", align_bytes=64, **kw)
-            scales = pool.tile([P, n], U8, name=name + "_scales", align_bytes=64, **kw)
+        def gate_col(r, block):
+            i = min(i for i in range(P)
+                    if GATE_STEP * i // (N * TOKEN_BLOCKS) == r and GATE_STEP * i % TOKEN_BLOCKS == block)
+            return gate_cols[:, i:i + 1]
+
+        def quantise(grouped, name):
+            n = grouped.shape[1] // PACK
+            codes = keep.tile([P, n], U32, name=name + "_codes", align_bytes=64)
+            scales = keep.tile([P, n], U8, name=name + "_scales", align_bytes=64)
             nc.vector.quantize_mx(out=codes[:].bitcast(FP8X4), scales=scales[:], in_=grouped)
             return codes, scales
 
         def group_wu(raw, m0, copy, grouped):
-            count = raw.shape[2] // 4
-            copy(out=grouped.rearrange("p (d m j) -> p m j d", d=4, j=4)[:, m0:m0 + count, :, :],
-                 in_=raw[:].rearrange("p j (m d) -> p m j d", d=4))
+            count = raw.shape[2] // PACK
+            copy(out=grouped.rearrange("p (d m j) -> p m j d", d=PACK, j=PACK)[:, m0:m0 + count, :, :],
+                 in_=raw[:].rearrange("p j (m d) -> p m j d", d=PACK))
 
         def group_u(i, copy):
             n = TOKEN_CHUNKS[i][1]
-            grouped = keep.tile([P, n, 4], BF16, name=f"u_grouped{i}", align_bytes=64)
-            copy(out=grouped[:].rearrange("p (c i) j -> p c j i", i=4), in_=u_raw[i][:].rearrange("p j (c i) -> p c j i", i=4))
+            grouped = keep.tile([P, n, PACK], BF16, name=f"u_grouped{i}", align_bytes=64)
+            copy(out=grouped[:].rearrange("p (c i) j -> p c j i", i=4),
+                 in_=u_raw[i][:].rearrange("p j (c i) -> p c j i", i=4))
             return grouped[:].rearrange("p t j -> p (t j)")
 
-        def project(a, wq, i, h, copy):
+        def project(a, wu_mx, i, h, copy):
             t0, n = TOKEN_CHUNKS[i]
             acc = bank("proj")
             for e in range(2):
                 cols = slice((2 * h + e) * P, (2 * h + e + 1) * P)
                 nc.tensor.matmul_mx(
                     out=acc[:, e * n:(e + 1) * n],
-                    lhsT=wq[0][:, cols].bitcast(FP8X4), lhsT_scale=wq[1][:, cols],
-                    rhs=uq[i][0][:].bitcast(FP8X4), rhs_scale=uq[i][1][:],
+                    lhsT=wu_mx[0][:, cols].bitcast(FP8X4), lhsT_scale=wu_mx[1][:, cols],
+                    rhs=u_mx[i][0][:].bitcast(FP8X4), rhs_scale=u_mx[i][1][:],
                     start=True, stop=True)
             copy(out=x_pairs[a, h][:, t0:t0 + n, :], in_=acc[:, 0:2 * n].rearrange("p (e t) -> p t e", e=2))
 
-        v_copy, s_copy = nc.vector.tensor_copy, nc.scalar.copy
-        wu0_grouped = keep.tile([P, 2048], BF16, align_bytes=64)
+        head_copies = (s_copy, v_copy, s_copy)
+        wu0_grouped = keep.tile([P, PACK * PASS], BF16, align_bytes=64)
         for i in range(2):
-            group_wu(wu_raw[i], 64 * i, v_copy, wu0_grouped[:])
-        wq0 = quantise(wu0_grouped[:], 512, "wu0", keep)
-        uq = []
-        for i, copy in enumerate((s_copy, v_copy, s_copy)):
-            uq.append(quantise(group_u(i, copy), TOKEN_CHUNKS[i][1], f"u{i}", keep))
-        for i, copy in enumerate((s_copy, v_copy, s_copy)):
-            project(0, wq0, i, 0, copy)
+            group_wu(wu0_raw[i], i * half // PACK, v_copy, wu0_grouped[:])
+        wu0_mx = quantise(wu0_grouped[:], "wu0")
+        u_mx = []
+        for i, copy in enumerate(head_copies):
+            u_mx.append(quantise(group_u(i, copy), f"u{i}"))
+        for i, copy in enumerate(head_copies):
+            project(0, wu0_mx, i, 0, copy)
         for i in range(len(TOKEN_CHUNKS)):
-            project(0, wq0, i, 1, s_copy)
+            project(0, wu0_mx, i, 1, s_copy)
 
-        y = [keep.tile([P, SLOTS], F32, name=f"y{nb}") for nb in range(N // P)]
+        y = [keep.tile([P, SLOTS], F32, name=f"y{nb}") for nb in range(ROW_BLOCKS)]
         starts = [sum(SLOT_CHUNKS[:c]) for c in range(len(SLOT_CHUNKS))]
-
         last = len(SLOT_CHUNKS) - 1
-        units = [(0, 0), (1, 0), (2, 0), (0, 1), (1, 1), (2, 1)]
-        for c in range(3, last + 1):
-            units.extend([(c, 0), (c, 1)])
-        between = {4: [(0, 0)], 5: [(1, 0)], 6: [(2, 0)], 7: [(0, 1)], 9: [(3, 0)]}
-        stage = [keep.tile([P, 2 * BANK], U32, name=f"stage{i}", align_bytes=64) for i in range(2)]
-        picked = [keep.tile([P, 3 * BANK], U32, name=f"picked{i}", align_bytes=64) for i in range(2)]
-        end = len(units) - 1
+
+        steps = [(c, a) for a in range(PASSES) for c in range(LEAD)]
+        steps.extend((c, a) for c in range(LEAD, last + 1) for a in range(PASSES))
+        end = len(steps) - 1
+        woven_ring = [keep.tile([P, 2 * BANK], U32, name=f"woven{i}", align_bytes=64) for i in range(2)]
+        picked_ring = [keep.tile([P, 2 * BANK], U32, name=f"picked{i}", align_bytes=64) for i in range(2)]
+        wu1_stage = keep.tile([P, 2 * BANK], U32, align_bytes=64)
+        slot_mx = {}
+
+        def picked(u):
+            return wu1_stage if u == LEAD - 1 else picked_ring[u % 2]
 
         def woven(u):
-            n = SLOT_CHUNKS[units[u][0]]
-            tile = picked[(end - 1) % 2] if u == end else stage[u % 2]
-            return tile[:, 0:2 * n]
-        xq = {}
+            n = SLOT_CHUNKS[steps[u][0]]
+            stage = picked(end - 1) if u == end else woven_ring[u % 2]
+            return stage[:, 0:2 * n]
 
         def gather(u):
-            c, a = units[u]
+            c, a = steps[u]
             s0, n = starts[c], SLOT_CHUNKS[c]
+            offsets = offs_sb[:, s0 // LIST_ROWS:(s0 + n) // LIST_ROWS]
             for h in range(2):
                 window = x_pairs[a, h][:].rearrange("p t e -> p (t e)").bitcast(U32)
-                nc.vector.tensor_copy(picked[u % 2][:, h * n:(h + 1) * n], window.indirect(offs_sb[:, s0 // 16:(s0 + n) // 16]))
+                nc.vector.tensor_copy(picked(u)[:, h * n:(h + 1) * n], window.indirect(offsets))
 
         def weave(u):
-            n = SLOT_CHUNKS[units[u][0]]
+            n = SLOT_CHUNKS[steps[u][0]]
             nc.scalar.copy(out=woven(u).rearrange("p (s h) -> p s h", h=2),
-                           in_=picked[u % 2][:, 0:2 * n].rearrange("p (h s) -> p s h", h=2))
+                           in_=picked(u)[:, 0:2 * n].rearrange("p (h s) -> p s h", h=2))
 
-        def quantise_unit(u):
-            c, a = units[u]
-            n = SLOT_CHUNKS[c]
-            xq[c, a] = quantise(woven(u).bitcast(BF16), n, f"slot{c}{a}", keep)
+        def quantise_step(u):
+            c, a = steps[u]
+            slot_mx[c, a] = quantise(woven(u).bitcast(BF16), f"slot{c}{a}")
 
-        def relu_tile():
-            tile = ring.tile([P, 2 * C], F32, name="relu")
-            return tile[:]
-
-        def experts(c, nb, first, second=None, on_vector=False):
+        def experts(c, nb, scratch, on_vector=False):
             s0, n = starts[c], SLOT_CHUNKS[c]
             acc = bank("expert")
             for i in range(n // C):
                 e = s0 // C + i
-                g, le = divmod(e, EXPERTS_PER_LOAD)
+                g, local = divmod(e, EXPERTS_PER_LOAD)
+                cols = slice(i * C, (i + 1) * C)
                 for a in range(PASSES):
                     nc.tensor.matmul_mx(
-                        out=acc[:, i * C:(i + 1) * C],
-                        lhsT=words[g][:, le * PASSES + a, nb * 2 * P:(nb + 1) * 2 * P].bitcast(FP4X4),
-                        lhsT_scale=planes[:, e * PASSES + a, nb * P:(nb + 1) * P],
-                        rhs=xq[c, a][0][:, i * C:(i + 1) * C].bitcast(FP8X4),
-                        rhs_scale=xq[c, a][1][:, i * C:(i + 1) * C],
+                        out=acc[:, cols],
+                        lhsT=w_word_sb[g][:, local * PASSES + a, nb * 2 * P:(nb + 1) * 2 * P].bitcast(FP4X4),
+                        lhsT_scale=w_scale_sb[:, e * PASSES + a, nb * P:(nb + 1) * P],
+                        rhs=slot_mx[c, a][0][:, cols].bitcast(FP8X4), rhs_scale=slot_mx[c, a][1][:, cols],
                         start=(a == 0), stop=(a == PASSES - 1))
-            halves = [first, relu_tile() if second is None else second] if n > 2 * C else [first]
+
+            def relus(first, count):
+                return scratch[first // (2 * C)][:, first % (2 * C):first % (2 * C) + count]
+
             for i in range(n // C):
                 e = s0 // C + i
-                relu = halves[i // 2][:, (i % 2) * C:(i % 2 + 1) * C]
+                sums, bias_col = acc[:, i * C:(i + 1) * C], bias[:, nb, e:e + 1]
                 if on_vector:
-                    nc.vector.tensor_scalar(relu, acc[:, i * C:(i + 1) * C], bias[:, nb, e:e + 1], 0.0,
-                                            mybir.AluOpType.add, mybir.AluOpType.max)
+                    nc.vector.tensor_scalar(relus(i * C, C), sums, bias_col, 0.0, ALU.add, ALU.max)
                 else:
-                    nc.scalar.activation(relu, acc[:, i * C:(i + 1) * C], ACT.Relu, bias=bias[:, nb, e:e + 1])
-            width = max(n // 2, C)
-            for i in range(n // width):
-                src = halves[i][:, 0:width] if n > 2 * C else first[:, i * width:(i + 1) * width]
-                dst = y[nb][:, s0 + i * width:s0 + (i + 1) * width]
+                    nc.scalar.activation(relus(i * C, C), sums, ACT.Relu, bias=bias_col)
+            width = n // 2
+            for first in (0, width):
+                src, dst = relus(first, width), y[nb][:, s0 + first:s0 + first + width]
                 if on_vector:
-                    nc.vector.tensor_tensor(dst, src, src, mybir.AluOpType.mult)
+                    nc.vector.tensor_tensor(dst, src, src, ALU.mult)
                 else:
                     nc.scalar.activation(dst, src, ACT.Square)
 
-        wq1_in = picked[1][:, BANK:3 * BANK].bitcast(BF16)
-        group_wu(wu_raw[2], 0, s_copy, wq1_in)
-        for u in range(len(units)):
-            if u == 1:
-                wq1 = quantise(wq1_in, 512, "wu1", keep)
+        behind_weave = {steps.index((c, 1)) + 1: (c, 0) for c in range(LEAD)}
+        behind_weave[steps.index((LEAD, 1))] = (0, 1)
+        behind_weave[steps.index((LEAD, 1)) + 2] = (LEAD, 0)
+
+        wu1_grouped = wu1_stage[:].bitcast(BF16)
+        group_wu(wu1_raw, 0, s_copy, wu1_grouped)
+        for u in range(len(steps)):
+            if u == LEAD - 1:
+                wu1_mx = quantise(wu1_grouped, "wu1")
                 for h in range(2):
                     for i in range(len(TOKEN_CHUNKS)):
-                        project(1, wq1, i, h, v_copy if (h, i) == (0, 9) else s_copy)
+                        project(1, wu1_mx, i, h, s_copy)
             gather(u)
             weave(u)
             if u > 0:
-                quantise_unit(u - 1)
-            for c, nb in between.get(u, []):
-                experts(c, nb, woven(u + 1).bitcast(F32))
-        spare = picked[end % 2][:].bitcast(F32)
-        experts(last - 1, 0, spare[:, 0:256])
-        quantise_unit(end)
-        experts(last, 0, spare[:, 256:512])
-        after = woven(end).bitcast(F32)
-        experts(3, 1, after[:, 0:256], after[:, 256:512], on_vector=True)
-        for c in (1, 2, 4, 5):
-            experts(c, 1, spare[:, 256:512], spare[:, 512:768])
+                quantise_step(u - 1)
+            if u in behind_weave:
+                more_relus = ring.tile([P, 2 * C], F32)
+                experts(*behind_weave[u], [woven(u + 1).bitcast(F32), more_relus])
 
-        groups = ((0, 4), (4, 1))
-        turn_banks = [[bank("turned0"), bank("turned1")], [bank("turned2"), bank("turned3")]]
+        spare = picked(end)[:].bitcast(F32)
+        spares = [spare[:, 0:2 * C], spare[:, 2 * C:4 * C]]
+        experts(last - 1, 0, spares[0:1])
+        quantise_step(end)
+        experts(last, 0, spares[1:2])
+        after = woven(end).bitcast(F32)
+        experts(LEAD, 1, [after[:, 0:2 * C], after[:, 2 * C:4 * C]], on_vector=True)
+        for i, c in enumerate(c for c in range(1, last + 1) if c != LEAD):
+            experts(c, 1, [spares[(i + 1) % 2], spares[i % 2]])
+
+        turned_choices = TOP - 1
+        turn_banks = [[bank(f"turned{gi}{i}") for i in range(2)] for gi in range(len(TOKEN_GROUPS))]
+        fetched = [keep.tile([P, T], F32, name=f"fetched{r}") for r in range(turned_choices)]
         products = keep.tile([P, T], F32)
-        fetch_ring = [keep.tile([P, T], F32, name=f"fetched{i}") for i in range(3)]
-        for nb in range(N // P):
-            final = True
-            turned_choices = TOP - 1
-            total = [bank(f"total{i}") for i in range(len(groups))]
+        for nb in range(ROW_BLOCKS):
+            total = [bank(f"total{gi}") for gi in range(len(TOKEN_GROUPS))]
             for r in range(turned_choices):
-                fetched = fetch_ring[r]
-                nc.vector.tensor_copy(fetched[:], y[nb][:].indirect(pos_sb[r][:]))
-                for gi, (first, count) in enumerate(groups):
-                    turned = turn_banks[gi][(nb * (TOP - 1) + r) % 2]
-                    for tb in range(count):
-                        nc.tensor.transpose(turned[:, tb * P:(tb + 1) * P],
-                                            fetched[:, (first + tb) * P:(first + tb + 1) * P], ident[:])
-                    weighted = ring.tile([P, BANK], F32, name="weighted")
-                    for tb in range(count):
-                        nc.scalar.activation(weighted[:, tb * P:(tb + 1) * P], turned[:, tb * P:(tb + 1) * P], ACT.Copy,
-                                             scale=gate_cols[:, first + tb, r:r + 1])
-                    for tb in range(count):
-                        nc.tensor.matmul(total[gi][:, tb * P:(tb + 1) * P], weighted[:, tb * P:(tb + 1) * P], ident[:],
-                                         start=(r == 0 and tb == 0), stop=(r == turned_choices - 1 and tb == count - 1),
+                nc.vector.tensor_copy(fetched[r][:], y[nb][:].indirect(pos_sb[r][:]))
+                for gi, (first, count) in enumerate(TOKEN_GROUPS):
+                    turned = turn_banks[gi][(nb * turned_choices + r) % 2]
+                    for i in range(count):
+                        nc.tensor.transpose(turned[:, i * P:(i + 1) * P],
+                                            fetched[r][:, (first + i) * P:(first + i + 1) * P], ident[:])
+                    weighted = ring.tile([P, BANK], F32)
+                    for i in range(count):
+                        nc.scalar.activation(weighted[:, i * P:(i + 1) * P], turned[:, i * P:(i + 1) * P], ACT.Copy,
+                                             scale=gate_col(r, first + i))
+                    for i in range(count):
+                        nc.tensor.matmul(total[gi][:, i * P:(i + 1) * P], weighted[:, i * P:(i + 1) * P], ident[:],
+                                         start=(r == 0 and i == 0), stop=(r == turned_choices - 1 and i == count - 1),
                                          is_transpose=True)
-            for gi, (first, count) in enumerate(groups):
+            for gi, (first, count) in enumerate(TOKEN_GROUPS):
                 t0, n = first * P, count * P
-                result = ring.tile([P, BANK], F32, name="result")
-                if final:
-                    product = products[:, t0:t0 + n]
-                    nc.vector.tensor_tensor(product, y[nb][:].indirect(pos_sb[TOP - 1][:, t0 // 16:(t0 + n) // 16]),
-                                            gate_last[:, t0:t0 + n], mybir.AluOpType.mult)
-                    nc.vector.tensor_tensor(result[:, 0:n], total[gi][:, 0:n], product, mybir.AluOpType.add)
-                else:
-                    nc.scalar.copy(out=result[:, 0:n], in_=total[gi][:, 0:n])
+                result = ring.tile([P, BANK], F32)
+                offsets = pos_sb[TOP - 1][:, t0 // LIST_ROWS:(t0 + n) // LIST_ROWS]
+                nc.vector.tensor_tensor(products[:, t0:t0 + n], y[nb][:].indirect(offsets), gate_last[:, t0:t0 + n],
+                                        ALU.mult)
+                nc.vector.tensor_tensor(result[:, 0:n], total[gi][:, 0:n], products[:, t0:t0 + n], ALU.add)
                 nc.sync.dma_start(out=out[nb * P:(nb + 1) * P, t0:t0 + n], in_=result[:, 0:n])

from contextlib import ExitStack

import concourse.mybir as mybir
from concourse.masks import make_identity

F32 = mybir.dt.float32
BF16 = mybir.dt.bfloat16
I32 = mybir.dt.int32
U32 = mybir.dt.uint32
U16 = mybir.dt.uint16
U8 = mybir.dt.uint8
FP8X4 = mybir.dt.float8_e4m3fn_x4
FP4X4 = mybir.dt.float4_e2m1fn_x4
ACT = mybir.ActivationFunctionType
ALU = mybir.AluOpType

P = 128
PACK = 4
PASS = P * PACK
LIST_ROWS = 16
BANK = 512
M, K, T, E, C, N, TOP = 512, 1024, 640, 20, 128, 256, 4
SLOTS = E * C
PASSES = K // PASS
ROW_BLOCKS = N // P
TOKEN_BLOCKS = T // P

TOKEN_CHUNKS = ((0, 256), (256, 256), (512, 128))
SLOT_CHUNKS = (512, 512, 512, 512, 256, 256)
LEAD = 3
WINDOW = 704
EXPERTS_PER_LOAD = 5
GATE_STEP = 36
TOKEN_GROUPS = ((0, 4), (4, 1))

FLOPS = 2 * M * K * T + 2 * K * N * SLOTS


def tile_moe_prv_lin_relu2_kernel(
    tc, uT, wu, w_words, w_scales, b, gate, offs, pos1, pos2, pos3, pos4, out
):
    nc = tc.nc
    with ExitStack() as ctx:
        keep = ctx.enter_context(tc.tile_pool(name="keep", bufs=1))
        ring = ctx.enter_context(tc.tile_pool(name="ring", bufs=3))
        psum = ctx.enter_context(tc.psum_pool(name="psum", bufs=8))
        v_copy, s_copy = nc.vector.tensor_copy, nc.scalar.copy

        def bank(name):
            return psum.tile([P, BANK], F32, name=name, tag="bank")

        w_scale_sb = keep.tile([P, E * PASSES, N], U8, align_bytes=64)
        nc.vector.memset(w_scale_sb[:].bitcast(I32), 0)
        gate_rows = keep.tile([P, P], F32)
        gate_pieces = gate.rearrange("r n (b t) -> (r n b) t", t=P)
        nc.sync.dma_start(out=gate_rows[:], in_=gate_pieces[0:GATE_STEP * P:GATE_STEP, :])
        ident = keep.tile([P, P], F32)
        make_identity(nc, ident[:])
        x_pairs = {}
        for a in range(PASSES):
            for h in range(2):
                x_pairs[a, h] = keep.tile([P, WINDOW, 2], BF16, name=f"x_pairs{a}{h}")
                nc.gpsimd.memset(x_pairs[a, h][:, T:, :], 0.0)

        wu_rows = wu.rearrange("(p j) k -> p j k", j=PACK)
        u_rows = uT.rearrange("(p j) t -> p j t", j=PACK)
        half = PASS // 2
        wu0_raw = [keep.tile([P, PACK, half], F32, name=f"wu0_raw{i}") for i in range(2)]
        wu1_raw = keep.tile([P, PACK, PASS], F32)
        u_raw = [keep.tile([P, PACK, n], F32, name=f"u_raw{i}") for i, (t0, n) in enumerate(TOKEN_CHUNKS)]
        for i in range(2):
            nc.sync.dma_start(out=wu0_raw[i][:], in_=wu_rows[:, :, half * i:half * (i + 1)])
        for i, (t0, n) in enumerate(TOKEN_CHUNKS):
            nc.sync.dma_start(out=u_raw[i][:], in_=u_rows[:, :, t0:t0 + n])
        offs_sb = keep.tile([P, SLOTS // LIST_ROWS], U16)
        nc.sync.dma_start(offs_sb[:], offs)
        nc.sync.dma_start(out=wu1_raw[:], in_=wu_rows[:, :, PASS:2 * PASS])
        bias = keep.tile([P, ROW_BLOCKS, E], F32)
        nc.sync.dma_start(out=bias[:], in_=b.rearrange("(nb p) e -> p nb e", p=P))

        scale_rows = w_scales.rearrange("e a (q r) n -> r q (e a) n", r=4)
        for r in range(4):
            nc.sync.dma_start(out=w_scale_sb[:].bitcast(I32)[r:P:32, :, :], in_=scale_rows[r].bitcast(I32))
        w_word_sb = []
        for g in range(E // EXPERTS_PER_LOAD):
            words = keep.tile([P, EXPERTS_PER_LOAD * PASSES, 2 * N], U8, name=f"words{g}", align_bytes=64)
            src = w_words[g * EXPERTS_PER_LOAD:(g + 1) * EXPERTS_PER_LOAD].rearrange("e a p c -> p (e a) c")
            nc.sync.dma_start(out=words[:].bitcast(I32), in_=src.bitcast(I32))
            w_word_sb.append(words)
        pos_sb = []
        for r, pos in enumerate((pos1, pos2, pos3, pos4)):
            pos_tile = keep.tile([P, T // LIST_ROWS], U16, name=f"pos_sb{r}")
            nc.sync.dma_start(pos_tile[:], pos)
            pos_sb.append(pos_tile)
        gate_last = keep.tile([P, T], F32)
        nc.sync.dma_start(out=gate_last[:], in_=gate[TOP - 1, N - P:N, :])

        gate_cols = keep.tile([P, P], F32)
        gate_turned = bank("gate_turned")
        nc.tensor.transpose(gate_turned[:, 0:P], gate_rows[:], ident[:])
        nc.scalar.activation(gate_cols[:], gate_turned[:, 0:P], ACT.Copy)

        def gate_col(r, block):
            i = min(i for i in range(P)
                    if GATE_STEP * i // (N * TOKEN_BLOCKS) == r and GATE_STEP * i % TOKEN_BLOCKS == block)
            return gate_cols[:, i:i + 1]

        def quantise(grouped, name):
            n = grouped.shape[1] // PACK
            codes = keep.tile([P, n], U32, name=name + "_codes", align_bytes=64)
            scales = keep.tile([P, n], U8, name=name + "_scales", align_bytes=64)
            nc.vector.quantize_mx(out=codes[:].bitcast(FP8X4), scales=scales[:], in_=grouped)
            return codes, scales

        def group_wu(raw, m0, copy, grouped):
            count = raw.shape[2] // PACK
            copy(out=grouped.rearrange("p (d m j) -> p m j d", d=PACK, j=PACK)[:, m0:m0 + count, :, :],
                 in_=raw[:].rearrange("p j (m d) -> p m j d", d=PACK))

        def group_u(i, copy):
            n = TOKEN_CHUNKS[i][1]
            grouped = keep.tile([P, n, PACK], BF16, name=f"u_grouped{i}", align_bytes=64)
            copy(out=grouped[:].rearrange("p (c i) j -> p c j i", i=4),
                 in_=u_raw[i][:].rearrange("p j (c i) -> p c j i", i=4))
            return grouped[:].rearrange("p t j -> p (t j)")

        def project(a, wu_mx, i, h, copy):
            t0, n = TOKEN_CHUNKS[i]
            acc = bank("proj")
            for e in range(2):
                cols = slice((2 * h + e) * P, (2 * h + e + 1) * P)
                nc.tensor.matmul_mx(
                    out=acc[:, e * n:(e + 1) * n],
                    lhsT=wu_mx[0][:, cols].bitcast(FP8X4), lhsT_scale=wu_mx[1][:, cols],
                    rhs=u_mx[i][0][:].bitcast(FP8X4), rhs_scale=u_mx[i][1][:],
                    start=True, stop=True)
            copy(out=x_pairs[a, h][:, t0:t0 + n, :], in_=acc[:, 0:2 * n].rearrange("p (e t) -> p t e", e=2))

        head_copies = (s_copy, v_copy, s_copy)
        wu0_grouped = keep.tile([P, PACK * PASS], BF16, align_bytes=64)
        for i in range(2):
            group_wu(wu0_raw[i], i * half // PACK, v_copy, wu0_grouped[:])
        wu0_mx = quantise(wu0_grouped[:], "wu0")
        u_mx = []
        for i, copy in enumerate(head_copies):
            u_mx.append(quantise(group_u(i, copy), f"u{i}"))
        for i, copy in enumerate(head_copies):
            project(0, wu0_mx, i, 0, copy)
        for i in range(len(TOKEN_CHUNKS)):
            project(0, wu0_mx, i, 1, s_copy)

        y = [keep.tile([P, SLOTS], F32, name=f"y{nb}") for nb in range(ROW_BLOCKS)]
        starts = [sum(SLOT_CHUNKS[:c]) for c in range(len(SLOT_CHUNKS))]
        last = len(SLOT_CHUNKS) - 1

        steps = [(c, a) for a in range(PASSES) for c in range(LEAD)]
        steps.extend((c, a) for c in range(LEAD, last + 1) for a in range(PASSES))
        end = len(steps) - 1
        woven_ring = [keep.tile([P, 2 * BANK], U32, name=f"woven{i}", align_bytes=64) for i in range(2)]
        picked_ring = [keep.tile([P, 2 * BANK], U32, name=f"picked{i}", align_bytes=64) for i in range(2)]
        wu1_stage = keep.tile([P, 2 * BANK], U32, align_bytes=64)
        slot_mx = {}

        def picked(u):
            return wu1_stage if u == LEAD - 1 else picked_ring[u % 2]

        def woven(u):
            n = SLOT_CHUNKS[steps[u][0]]
            stage = picked(end - 1) if u == end else woven_ring[u % 2]
            return stage[:, 0:2 * n]

        def gather(u):
            c, a = steps[u]
            s0, n = starts[c], SLOT_CHUNKS[c]
            offsets = offs_sb[:, s0 // LIST_ROWS:(s0 + n) // LIST_ROWS]
            for h in range(2):
                window = x_pairs[a, h][:].rearrange("p t e -> p (t e)").bitcast(U32)
                nc.vector.tensor_copy(picked(u)[:, h * n:(h + 1) * n], window.indirect(offsets))

        def weave(u):
            n = SLOT_CHUNKS[steps[u][0]]
            nc.scalar.copy(out=woven(u).rearrange("p (s h) -> p s h", h=2),
                           in_=picked(u)[:, 0:2 * n].rearrange("p (h s) -> p s h", h=2))

        def quantise_step(u):
            c, a = steps[u]
            slot_mx[c, a] = quantise(woven(u).bitcast(BF16), f"slot{c}{a}")

        def experts(c, nb, scratch, on_vector=False):
            s0, n = starts[c], SLOT_CHUNKS[c]
            acc = bank("expert")
            for i in range(n // C):
                e = s0 // C + i
                g, local = divmod(e, EXPERTS_PER_LOAD)
                cols = slice(i * C, (i + 1) * C)
                for a in range(PASSES):
                    nc.tensor.matmul_mx(
                        out=acc[:, cols],
                        lhsT=w_word_sb[g][:, local * PASSES + a, nb * 2 * P:(nb + 1) * 2 * P].bitcast(FP4X4),
                        lhsT_scale=w_scale_sb[:, e * PASSES + a, nb * P:(nb + 1) * P],
                        rhs=slot_mx[c, a][0][:, cols].bitcast(FP8X4), rhs_scale=slot_mx[c, a][1][:, cols],
                        start=(a == 0), stop=(a == PASSES - 1))

            def relus(first, count):
                return scratch[first // (2 * C)][:, first % (2 * C):first % (2 * C) + count]

            for i in range(n // C):
                e = s0 // C + i
                sums, bias_col = acc[:, i * C:(i + 1) * C], bias[:, nb, e:e + 1]
                if on_vector:
                    nc.vector.tensor_scalar(relus(i * C, C), sums, bias_col, 0.0, ALU.add, ALU.max)
                else:
                    nc.scalar.activation(relus(i * C, C), sums, ACT.Relu, bias=bias_col)
            width = n // 2
            for first in (0, width):
                src, dst = relus(first, width), y[nb][:, s0 + first:s0 + first + width]
                if on_vector:
                    nc.vector.tensor_tensor(dst, src, src, ALU.mult)
                else:
                    nc.scalar.activation(dst, src, ACT.Square)

        behind_weave = {steps.index((c, 1)) + 1: (c, 0) for c in range(LEAD)}
        behind_weave[steps.index((LEAD, 1))] = (0, 1)
        behind_weave[steps.index((LEAD, 1)) + 2] = (LEAD, 0)

        wu1_grouped = wu1_stage[:].bitcast(BF16)
        group_wu(wu1_raw, 0, s_copy, wu1_grouped)
        for u in range(len(steps)):
            if u == LEAD - 1:
                wu1_mx = quantise(wu1_grouped, "wu1")
                for h in range(2):
                    for i in range(len(TOKEN_CHUNKS)):
                        project(1, wu1_mx, i, h, s_copy)
            gather(u)
            weave(u)
            if u > 0:
                quantise_step(u - 1)
            if u in behind_weave:
                more_relus = ring.tile([P, 2 * C], F32)
                experts(*behind_weave[u], [woven(u + 1).bitcast(F32), more_relus])

        spare = picked(end)[:].bitcast(F32)
        spares = [spare[:, 0:2 * C], spare[:, 2 * C:4 * C]]
        experts(last - 1, 0, spares[0:1])
        quantise_step(end)
        experts(last, 0, spares[1:2])
        after = woven(end).bitcast(F32)
        experts(LEAD, 1, [after[:, 0:2 * C], after[:, 2 * C:4 * C]], on_vector=True)
        for i, c in enumerate(c for c in range(1, last + 1) if c != LEAD):
            experts(c, 1, [spares[(i + 1) % 2], spares[i % 2]])

        turned_choices = TOP - 1
        turn_banks = [[bank(f"turned{gi}{i}") for i in range(2)] for gi in range(len(TOKEN_GROUPS))]
        fetched = [keep.tile([P, T], F32, name=f"fetched{r}") for r in range(turned_choices)]
        products = keep.tile([P, T], F32)
        for nb in range(ROW_BLOCKS):
            total = [bank(f"total{gi}") for gi in range(len(TOKEN_GROUPS))]
            for r in range(turned_choices):
                nc.vector.tensor_copy(fetched[r][:], y[nb][:].indirect(pos_sb[r][:]))
                for gi, (first, count) in enumerate(TOKEN_GROUPS):
                    turned = turn_banks[gi][(nb * turned_choices + r) % 2]
                    for i in range(count):
                        nc.tensor.transpose(turned[:, i * P:(i + 1) * P],
                                            fetched[r][:, (first + i) * P:(first + i + 1) * P], ident[:])
                    weighted = ring.tile([P, BANK], F32)
                    for i in range(count):
                        nc.scalar.activation(weighted[:, i * P:(i + 1) * P], turned[:, i * P:(i + 1) * P], ACT.Copy,
                                             scale=gate_col(r, first + i))
                    for i in range(count):
                        nc.tensor.matmul(total[gi][:, i * P:(i + 1) * P], weighted[:, i * P:(i + 1) * P], ident[:],
                                         start=(r == 0 and i == 0), stop=(r == turned_choices - 1 and i == count - 1),
                                         is_transpose=True)
            for gi, (first, count) in enumerate(TOKEN_GROUPS):
                t0, n = first * P, count * P
                result = ring.tile([P, BANK], F32)
                offsets = pos_sb[TOP - 1][:, t0 // LIST_ROWS:(t0 + n) // LIST_ROWS]
                nc.vector.tensor_tensor(products[:, t0:t0 + n], y[nb][:].indirect(offsets), gate_last[:, t0:t0 + n],
                                        ALU.mult)
                nc.vector.tensor_tensor(result[:, 0:n], total[gi][:, 0:n], products[:, t0:t0 + n], ALU.add)
                nc.sync.dma_start(out=out[nb * P:(nb + 1) * P, t0:t0 + n], in_=result[:, 0:n])
